import numpy as np
import ml_dtypes


def mxq(x, axis, fmt="e4m3"):
    dtype, down = {"e4m3": (ml_dtypes.float8_e4m3fn, 7), "e5m2": (ml_dtypes.float8_e5m2, 14)}[fmt]
    v = np.moveaxis(np.asarray(x, np.float32).astype(ml_dtypes.bfloat16).astype(np.float64), axis, -1)
    blocks = v.reshape(v.shape[:-1] + (-1, 32))
    amax = np.abs(blocks).max(-1, keepdims=True)
    byte = np.maximum(np.where(amax > 0, np.frexp(amax)[1] - 1 + 127, 0) - down, 1)
    scale = np.exp2(byte - 127.0)
    codes = (blocks / scale).astype(np.float32).astype(dtype).astype(np.float64)
    return np.moveaxis((codes * scale).reshape(v.shape), -1, axis)


WIDE = False


def mx_kscale(k):
    if not WIDE:
        return np.ones(k)
    levels = np.array([10, -10, 5, -5, 0])
    if k % 512:
        return np.exp2(np.random.permutation(np.resize(levels, k // 32))).repeat(32)
    a = np.empty((k // 512, 16))
    for p in range(k // 512):
        a[p, :8] = np.random.permutation(np.resize(levels, 8))
        for g in range(8):
            far = levels[np.abs(levels - a[p, g]) >= 10]
            a[p, g + 8] = far[np.random.randint(len(far))]
    return np.exp2(a.ravel()).repeat(32)


def f64(x):
    return np.asarray(x).astype(np.float64)


def striped(idx):
    return np.tile(idx.reshape(-1, 16).T, (8, 1)).astype(np.uint16)


def unstriped(offs):
    return offs[:16].T.reshape(-1).astype(np.int64)


E2M1 = np.array([0.0, 0.5, 1.0, 1.5, 2.0, 3.0, 4.0, 6.0, -0.0, -0.5, -1.0, -1.5, -2.0, -3.0, -4.0, -6.0])


def pack_weight(w, fmt):
    k, n = w.shape
    w = f64(np.asarray(w, np.float32).astype(ml_dtypes.bfloat16)).reshape(k // 32, 32, n)
    amax = np.abs(w).max(1)
    if fmt == "e4m3":
        byte = np.frexp(amax)[1] - 1 + 127 - 7
    else:
        mant, ex = np.frexp(amax / 6.0)
        byte = np.where(mant > 0.5, ex, ex - 1) + 127
    byte = np.clip(np.where(amax > 0, byte, 1), 1, 254)
    scaled = (w * np.exp2(127.0 - byte)[:, None, :]).reshape(k, n).astype(np.float32)
    by_word = np.ascontiguousarray(scaled.reshape(k // 512, 128, 4, n).transpose(0, 1, 3, 2))
    if fmt == "e4m3":
        words = by_word.astype(ml_dtypes.float8_e4m3fn).view(np.uint8)
    else:
        c = by_word.astype(ml_dtypes.float4_e2m1fn).view(np.uint8) & 0xF
        words = (c[..., 0::2] | (c[..., 1::2] << 4)).reshape(k // 512, 128, 2 * n)
    return np.ascontiguousarray(words), np.ascontiguousarray(byte.astype(np.uint8).reshape(k // 512, 16, n))


def unpack_weight(words, scales, fmt):
    g, _, n = scales.shape
    words = np.ascontiguousarray(words).reshape(g, 128, n, -1)
    if fmt == "e4m3":
        vals = words.view(ml_dtypes.float8_e4m3fn).astype(np.float64)
    else:
        nib = np.empty((g, 128, n, 4), np.uint8)
        nib[..., 0::2] = words & 0xF
        nib[..., 1::2] = words >> 4
        vals = E2M1[nib]
    vals = vals * np.repeat(np.exp2(scales.astype(np.float64) - 127.0), 8, axis=1)[..., None]
    return vals.transpose(0, 1, 3, 2).reshape(g * 512, n)


K, T, E, C, H, N = 512, 640, 10, 128, 512, 1024


def by_expert(wq, xq):
    return np.concatenate([wq[e].T @ xq[:, e * C:(e + 1) * C] for e in range(E)], axis=1)


def setup_inputs():
    n = np.random.standard_normal
    v = mx_kscale(N)
    u = mx_kscale(H)
    first = np.random.permutation(np.repeat(np.arange(E), T // E))
    second = (first + 1 + np.random.permutation(np.repeat(np.arange(E - 1), -(-T // (E - 1)))[:T])) % E
    while np.bincount(second, minlength=E).max() != T // E:
        load = np.bincount(second, minlength=E); hi, lo = int(load.argmax()), int(load.argmin())
        t = np.flatnonzero((second == hi) & (first != lo))[0]; second[t] = lo
    slot_token = np.empty(E * C, np.int64); pos = np.empty((2, T), np.int64); fill = np.zeros(E, np.int64)
    place = np.stack([np.random.permutation(C) for _ in range(E)])
    for r, deal in enumerate((first, second)):
        for t in np.random.permutation(T):
            e = deal[t]; j = e * C + place[e, fill[e]]; fill[e] += 1; slot_token[j] = t; pos[r, t] = j
    g = np.random.uniform(0.2, 0.8, T)
    w_slot = np.empty(E * C); w_slot[pos[0]] = g; w_slot[pos[1]] = 1.0 - g
    dy = pack_weight(n((N, T)) * v[:, None], "e4m3")
    return {
        "dy_words": dy[0],
        "dy_scales": dy[1],
        "wt": (n((N, K)) / np.sqrt(N) / v[:, None]).astype(np.float32),
        "wbt": (n((E, N, H)) / np.sqrt(N) / v[None, :, None] * u).astype(np.float32),
        "wat": (n((E, H, K)) / np.sqrt(H) / u[None, :, None]).astype(np.float32),
        "gate": (np.tile(w_slot, (128, 1))).astype(np.float32),
        "offs": striped(slot_token),
        "pos1": striped(pos[0]),
        "pos2": striped(pos[1]),
    }


def reference(dy_words, dy_scales, wt, wbt, wat, gate, offs, pos1, pos2):
    wtq = mxq(f64(wt), 0, "e4m3")
    wbtq = mxq(f64(wbt), 1, "e4m3")
    watq = mxq(f64(wat), 1, "e4m3")
    idx = unstriped(offs)
    dy = unpack_weight(dy_words, dy_scales, "e4m3")
    base = wtq.T @ dy
    dh = f64(gate[:1]) * by_expert(wbtq, dy[:, idx])
    dx = by_expert(watq, mxq(dh, 0, "e4m3"))
    c = dx[:, unstriped(pos1)] + dx[:, unstriped(pos2)]
    return base + c

@@ -1,0 +1,352 @@
+from contextlib import ExitStack
+
+import concourse.mybir as mybir
+from concourse.masks import make_identity
+
+K, T, E, C, H, N = 512, 640, 10, 128, 512, 1024
+SLOTS = E * C
+FLOPS = 2 * (N * K * T + N * H * SLOTS + H * K * SLOTS)
+
+F32 = mybir.dt.float32
+BF16 = mybir.dt.bfloat16
+I32 = mybir.dt.int32
+U32 = mybir.dt.uint32
+U16 = mybir.dt.uint16
+U8 = mybir.dt.uint8
+FP8X4 = mybir.dt.float8_e4m3fn_x4
+COPY = mybir.ActivationFunctionType.Copy
+ADD = mybir.AluOpType.add
+
+P = 128
+PACK = 4
+PASSES = N // (P * PACK)
+CHUNKS = K // P
+LIST_COL = 16
+PAIR = 2 * C
+PAIRS = E // 2
+BANK = 512
+TAIL = T - BANK
+SCALE_ROWS = 4
+
+STAGE_BUFS = 16
+WB_SCALAR_COLS = (0, H)
+LAST_WB_SCALAR_COLS = (0, 512)
+LATE_TURN_ON_SCALAR = (1, 1)
+FIRST_DX_ON_VECTOR = (0, 0, 1)
+FIRST_CHUNK_SCALAR_COLS = (0, 128, 0, 64, 128)
+DX_AFTER = (None, 30, 35, 40)
+
+
+def round_and_interleave(nc, grouped, raw, scalar_cols):
+    width = raw.shape[2]
+    shares = ((nc.scalar.copy, 0, scalar_cols), (nc.vector.tensor_copy, scalar_cols, width))
+    for copy, first, last in shares:
+        if first < last:
+            copy(
+                out=grouped[:, first:last, :].rearrange("p (c i) t -> p c t i", i=4),
+                in_=raw[:, :, first:last].rearrange("p t (c i) -> p c t i", i=4),
+            )
+
+
+def quantize(nc, codes, scales, grouped):
+    nc.vector.quantize_mx(out=codes.bitcast(FP8X4), scales=scales, in_=grouped.rearrange("p c t -> p (c t)"))
+
+
+def tile_moe_adb_none_kernel(
+    tc, dy_words, dy_scales, wt, wbt, wat, gate, offs, pos1, pos2, out
+):
+    nc = tc.nc
+    with ExitStack() as ctx:
+        keep = ctx.enter_context(tc.tile_pool(name="keep", bufs=1))
+        stage = ctx.enter_context(tc.tile_pool(name="stage", bufs=1))
+        work = ctx.enter_context(tc.tile_pool(name="work", bufs=2))
+        psum = ctx.enter_context(tc.psum_pool(name="psum", bufs=2))
+
+        slot_list = keep.tile([P, SLOTS // LIST_COL], U16, name="slot_list")
+        token_lists = [keep.tile([P, T // LIST_COL], U16, name="token_list%d" % r) for r in range(2)]
+        dy_w = keep.tile([P, PASSES, T], I32, name="dy_w", align_bytes=64)
+        dy_s = keep.tile([P, T], U8, name="dy_s", align_bytes=64)
+        dh_codes = keep.tile([P, SLOTS], U32, name="dh_codes", align_bytes=64)
+        dh_scales = keep.tile([P, SLOTS], U8, name="dh_scales", align_bytes=64)
+        ident = keep.tile([P, P], F32, name="ident")
+        gate_rows = keep.tile([P, P], F32, name="gate_rows")
+        gate_cols = keep.tile([P, E], F32, name="gate_cols")
+
+        places = []
+
+        def staged(shape, dtype, name):
+            places.append("place%d" % (len(places) % STAGE_BUFS))
+            return stage.tile(shape, dtype, name=name, tag=places[-1], align_bytes=64)
+
+        def after(place, shape, dtype, name):
+            return stage.tile(shape, dtype, name=name, tag=places[place], align_bytes=64)
+
+        nc.vector.memset(dy_s[:].bitcast(I32), 0)
+        make_identity(nc, ident[:])
+
+        nc.sync.dma_start(out=slot_list[:], in_=offs)
+        nc.sync.dma_start(out=dy_w[:], in_=dy_words.rearrange("s p t d -> p s (t d)").bitcast(I32))
+        for q in range(4):
+            nc.sync.dma_start(
+                out=dy_s[32 * q : 32 * q + PASSES * SCALE_ROWS, :].bitcast(I32),
+                in_=dy_scales[:, SCALE_ROWS * q : SCALE_ROWS * (q + 1), :].bitcast(I32),
+            )
+        small_loads = [
+            (gate_rows[:], gate.rearrange("r (e u) -> (r e) u", u=C)[0:P, :]),
+            (token_lists[0][:], pos1),
+            (token_lists[1][:], pos2),
+        ]
+
+        def load_wb(e, s):
+            raw = staged([P, PACK, H], F32, "wb_raw")
+            nc.sync.dma_start(out=raw[:], in_=wbt[e].rearrange("(s p j) w -> s p j w", s=PASSES, j=PACK)[s])
+            return raw[:]
+
+        def load_wa(c, first, last):
+            raw = staged([P, PACK, (last - first) * P], F32, "wa_raw")
+            for e in range(first, last):
+                nc.sync.dma_start(
+                    out=raw[:, :, (e - first) * P : (e - first + 1) * P],
+                    in_=wat[e].rearrange("(p j) k -> p j k", j=PACK)[:, :, c * P : (c + 1) * P],
+                )
+            return [raw[:, :, i * PAIR : (i + 1) * PAIR] for i in range((last - first) // 2)]
+
+        def load_wt(h):
+            raw = [staged([P, PACK, 2 * P], F32, "wt_raw") for s in range(PASSES)]
+            for s in range(PASSES):
+                nc.sync.dma_start(
+                    out=raw[s][:],
+                    in_=wt.rearrange("(s p j) k -> s p j k", s=PASSES, j=PACK)[s, :, :, h * 2 * P : (h + 1) * 2 * P],
+                )
+            return [piece[:] for piece in raw]
+
+        def rounded(raw, scalar_cols, name, bufs=4):
+            grouped = work.tile([P, raw.shape[2], PACK], BF16, name=name, bufs=bufs, align_bytes=64)
+            round_and_interleave(nc, grouped[:], raw, scalar_cols)
+            return grouped[:]
+
+        def quantized(grouped, name):
+            codes = work.tile([P, grouped.shape[1]], U32, name=name + "_codes", bufs=4, align_bytes=64)
+            scales = work.tile([P, grouped.shape[1]], U8, name=name + "_scales", bufs=4, align_bytes=64)
+            quantize(nc, codes[:], scales[:], grouped)
+            return codes, scales
+
+        slot_w, slot_s = {}, {}
+
+        def entries(g):
+            return slot_list[:, g * PAIR // LIST_COL : (g + 1) * PAIR // LIST_COL]
+
+        def slot_tile(g, back, shape, dtype, name):
+            if g < 2:
+                return work.tile(shape, dtype, name=name, align_bytes=64)
+            return after(PASSES * (2 * g - back), shape, dtype, name)
+
+        def gather_words(g):
+            slot_w[g] = slot_tile(g, 1, [P, PASSES, PAIR], U32, "slot_w")
+            for s in range(PASSES):
+                nc.vector.tensor_copy(out=slot_w[g][:, s, :], in_=dy_w[:, s, :].bitcast(U32).indirect(entries(g)))
+
+        def gather_scales(g):
+            slot_s[g] = slot_tile(g, 2, [P, PAIR], U8, "slot_s")
+            nc.vector.tensor_copy(out=slot_s[g][:], in_=dy_s[:].indirect(entries(g)))
+
+        def first_product(e, s, acc, operand):
+            slots = slice(e % 2 * C, (e % 2 + 1) * C)
+            codes, scales = operand
+            nc.tensor.matmul_mx(
+                out=acc[:],
+                lhsT=slot_w[e // 2][:, s, slots].bitcast(FP8X4),
+                lhsT_scale=slot_s[e // 2][SCALE_ROWS * s : P, slots],
+                rhs=codes[:].bitcast(FP8X4),
+                rhs_scale=scales[:],
+                start=(s == 0),
+                stop=(s == PASSES - 1),
+            )
+
+        def gate_and_turn(e, acc):
+            if e + 1 < E:
+                dh_rows = after(PASSES * (e + 1) + 1, [P, 2, P, 2], BF16, "dh_rows")
+            else:
+                dh_rows = work.tile([P, 2, P, 2], BF16, name="dh_rows", bufs=1, align_bytes=64)
+            nc.scalar.activation(
+                out=dh_rows[:],
+                in_=acc[:].rearrange("j (p u v) -> j u p v", u=2, v=2),
+                func=COPY,
+                scale=gate_cols[:, e : e + 1],
+            )
+            pairs = dh_rows[:].rearrange("j u p v -> j (u p v)").bitcast(F32)
+            turned = psum.tile([P, 2, C], F32, name="turned", tag="turn")
+            for u in range(2):
+                nc.tensor.transpose(turned[:, u, :], pairs[:, u * P : (u + 1) * P], ident[:])
+            return turned
+
+        def leave_turned(e, turned):
+            dh_bf = work.tile([P, C, PACK], BF16, name="dh_bf", align_bytes=64)
+            (nc.scalar.copy if e >= E - 2 and LATE_TURN_ON_SCALAR[e - E + 2] else nc.vector.tensor_copy)(
+                out=dh_bf[:].rearrange("p j t -> p (j t)").bitcast(F32).rearrange("p (j u) -> p j u", u=2),
+                in_=turned[:].rearrange("p u j -> p j u"),
+            )
+            return dh_bf
+
+        def quantize_dh(e, dh_bf):
+            slots = slice(e * C, (e + 1) * C)
+            quantize(nc, dh_codes[:, slots], dh_scales[:, slots], dh_bf[:])
+
+        for g in range(2):
+            gather_words(g)
+            gather_scales(g)
+        sums = {}
+        for e in range(E):
+            raw = [load_wb(e, s) for s in range(PASSES)]
+            if e < len(small_loads):
+                nc.sync.dma_start(out=small_loads[e][0], in_=small_loads[e][1])
+            if e == 0:
+                gate_t = psum.tile([P, P], F32, name="gate_t", tag="turn")
+                nc.tensor.transpose(gate_t[:], gate_rows[:], ident[:])
+            sums[e] = psum.tile([P, H], F32, name="acc", tag="acc", bufs=6)
+            grouped = rounded(raw[0], (LAST_WB_SCALAR_COLS if e == E - 1 else WB_SCALAR_COLS)[0], "wb_bf")
+            if e > 1:
+                dh_bf = leave_turned(e - 2, turned)
+            first_product(e, 0, sums[e], quantized(grouped, "wb"))
+            if e > 1:
+                quantize_dh(e - 2, dh_bf)
+            if 2 <= e // 2 + 1 < PAIRS:
+                (gather_words if e % 2 else gather_scales)(e // 2 + 1)
+            grouped = rounded(raw[1], (LAST_WB_SCALAR_COLS if e == E - 1 else WB_SCALAR_COLS)[1], "wb_bf")
+            if e == 0:
+                nc.scalar.activation(out=gate_cols[:], in_=gate_t[:, 0:E], func=COPY)
+            first_product(e, 1, sums[e], quantized(grouped, "wb"))
+            if e > 0:
+                turned = gate_and_turn(e - 1, sums[e - 1])
+        quantize_dh(E - 2, leave_turned(E - 2, turned))
+
+        banks, dx, pair_sum = {}, {}, {}
+
+        def second_product(c, g, grouped):
+            codes, scales = quantized(grouped, "wa")
+            if g % 2 == 0:
+                banks[c, g // 2] = psum.tile([P, BANK], F32, name="dx_bank", tag="acc", bufs=6)
+            for i in range(2):
+                cols = slice(i * P, (i + 1) * P)
+                slots = slice(g * PAIR + i * C, g * PAIR + (i + 1) * C)
+                place = (g % 2) * PAIR + i * C
+                nc.tensor.matmul_mx(
+                    out=banks[c, g // 2][:, place : place + C],
+                    lhsT=codes[:, cols].bitcast(FP8X4),
+                    lhsT_scale=scales[:, cols],
+                    rhs=dh_codes[:, slots].bitcast(FP8X4),
+                    rhs_scale=dh_scales[:, slots],
+                    start=True,
+                    stop=True,
+                )
+
+        def leave_dx(c, b):
+            copy = nc.vector.tensor_copy if c == 0 and FIRST_DX_ON_VECTOR[b] else nc.scalar.copy
+            width = min(BANK, SLOTS - b * BANK)
+            if b == 0 and c == 0:
+                dx[c] = keep.tile([P, SLOTS], F32, name="dx")
+            elif b == 0:
+                dx[c] = after(DX_AFTER[c], [P, SLOTS], F32, "dx")
+            copy(out=dx[c][:, b * BANK : b * BANK + width], in_=banks[c, b][:, 0:width])
+
+        picked = {}
+
+        def pick(c, r):
+            if r == 0:
+                picked[c] = work.tile([P, 2, T], F32, name="picked")
+            nc.vector.tensor_copy(out=picked[c][:, r, :], in_=dx[c][:].indirect(token_lists[r][:]))
+
+        def add_picked(c):
+            pair_sum[c] = work.tile([P, T], F32, name="pair_sum", tag="late%d" % c, bufs=1, align_bytes=64)
+            nc.vector.tensor_tensor(out=pair_sum[c][:], in0=picked[c][:, 0, :], in1=picked[c][:, 1, :], op=ADD)
+
+        def load_chunk(c):
+            return [load_wa(c, 2 * g, 2 * g + 2)[0] for g in range(PAIRS)]
+
+        raw = load_chunk(0)
+        bf = [rounded(raw[0], FIRST_CHUNK_SCALAR_COLS[0], "wa_bf")]
+        turned = gate_and_turn(E - 1, sums[E - 1])
+        bf.append(rounded(raw[1], FIRST_CHUNK_SCALAR_COLS[1], "wa_bf"))
+        second_product(0, 0, bf[0])
+        dh_bf = leave_turned(E - 1, turned)
+        bf.append(rounded(raw[2], FIRST_CHUNK_SCALAR_COLS[2], "wa_bf"))
+        second_product(0, 1, bf[1])
+        quantize_dh(E - 1, dh_bf)
+        bf.append(rounded(raw[3], FIRST_CHUNK_SCALAR_COLS[3], "wa_bf"))
+        leave_dx(0, 0)
+        second_product(0, 2, bf[2])
+        bf.append(rounded(raw[4], FIRST_CHUNK_SCALAR_COLS[4], "wa_bf"))
+        second_product(0, 3, bf[3])
+        second_product(0, 4, bf[4])
+        leave_dx(0, 1)
+
+        leave_dx(0, 2)
+        raw = load_chunk(1)
+        ahead = rounded(raw[0], PAIR, "wa_bf")
+        for c in range(1, CHUNKS):
+            second_product(c, 0, ahead)
+            bf = [ahead] + [rounded(raw[g], PAIR, "wa_bf") for g in (1, 2, 3)]
+            pick(c - 1, 0)
+            second_product(c, 1, bf[1])
+            pick(c - 1, 1)
+            second_product(c, 2, bf[2])
+            bf.append(rounded(raw[4], 0, "late%d" % (c - 1), bufs=1))
+            second_product(c, 3, bf[3])
+            second_product(c, 4, bf[4])
+            if c + 1 < CHUNKS:
+                raw = load_chunk(c + 1)
+                ahead = rounded(raw[0], PAIR, "wa_bf")
+            else:
+                raw = load_wt(0) + load_wt(1)
+                wt_bf = [rounded(piece, 2 * P, "wa_bf") for piece in raw[0:1]]
+            for b in range(3):
+                leave_dx(c, b)
+            add_picked(c - 1)
+
+        base = {}
+
+        def frozen_pass(h, s, operand):
+            codes, scales = operand
+            for i in range(2):
+                c = 2 * h + i
+                cols = slice(i * P, (i + 1) * P)
+                if s == 0:
+                    wide = psum.tile([P, BANK], F32, name="acc", tag="acc", bufs=6)
+                    if h == 0:
+                        narrow = psum.tile([P, TAIL], F32, name="narrow", tag="turn")
+                    else:
+                        narrow = psum.tile([P, TAIL], F32, name="narrow", tag="acc", bufs=6)
+                    base[c] = (wide[:], narrow[:])
+                for target, tokens in zip(base[c], (slice(0, BANK), slice(BANK, T))):
+                    nc.tensor.matmul_mx(
+                        out=target,
+                        lhsT=codes[:, cols].bitcast(FP8X4),
+                        lhsT_scale=scales[:, cols],
+                        rhs=dy_w[:, s, tokens].bitcast(FP8X4),
+                        rhs_scale=dy_s[SCALE_ROWS * s : P, tokens],
+                        start=(s == 0),
+                        stop=(s == PASSES - 1),
+                    )
+
+        def finish(c):
+            if c == 0:
+                result = after(DX_AFTER[last], [P, T], F32, "result")
+            elif c == 1:
+                result = work.tile([P, T], F32, name="result", tag="last_bf", bufs=1, align_bytes=64)
+            else:
+                result = work.tile([P, T], F32, name="result")
+            for part, tokens in zip(base[c], (slice(0, BANK), slice(BANK, T))):
+                nc.vector.tensor_tensor(out=result[:, tokens], in0=part, in1=pair_sum[c][:, tokens], op=ADD)
+            nc.sync.dma_start(out=out[c * P : (c + 1) * P, :], in_=result[:])
+
+        last = CHUNKS - 1
+        bf = wt_bf + [rounded(piece, 2 * P, "wa_bf") for piece in raw[1:3]] + [rounded(raw[3], 2 * P, "last_bf", bufs=1)]
+        frozen_pass(0, 0, quantized(bf[0], "wa"))
+        pick(last, 0)
+        frozen_pass(0, 1, quantized(bf[1], "wa"))
+        pick(last, 1)
+        frozen_pass(1, 0, quantized(bf[2], "wa"))
+        frozen_pass(1, 1, quantized(bf[3], "wa"))
+        add_picked(last)
+        for c in range(CHUNKS):
+            finish(c)

@@ -31,10 +31,14 @@ SCALE_ROWS = 4
 STAGE_BUFS = 16
 WB_SCALAR_COLS = (0, H)
 LAST_WB_SCALAR_COLS = (0, 512)
-LATE_TURN_ON_SCALAR = (1, 1)
-FIRST_DX_ON_VECTOR = (0, 0, 1)
-FIRST_CHUNK_SCALAR_COLS = (0, 128, 0, 64, 128)
-DX_AFTER = (None, 30, 35, 40)
+LATE_TURN_ON_SCALAR = (1, 0)
+HALF_SHARE = (2, 2, 0, 3, 0, 4, 1, 2, 4, 0)
+HALF_DX_ON_VECTOR = (0, 1, 1, 0, 0)
+UNIT_SHARE = (0, 3, 4, 4, 2, 4, 3, 3, 3, 4, 4, 2, 3, 4)
+DX_AFTER = (35, 39)
+HOLD_SUM = (3, 4, 9)
+HOLD_RESULT = (1, 1)
+PICK_AT = (0, 1, 2, 4, 5, 7, 9, 12)
 
 
 def round_and_interleave(nc, grouped, raw, scalar_cols):
@@ -136,18 +140,13 @@ def tile_moe_adb_none_kernel(
         def entries(g):
             return slot_list[:, g * PAIR // LIST_COL : (g + 1) * PAIR // LIST_COL]
 
-        def slot_tile(g, back, shape, dtype, name):
-            if g < 2:
-                return work.tile(shape, dtype, name=name, align_bytes=64)
-            return after(PASSES * (2 * g - back), shape, dtype, name)
-
         def gather_words(g):
-            slot_w[g] = slot_tile(g, 1, [P, PASSES, PAIR], U32, "slot_w")
+            slot_w[g] = work.tile([P, PASSES, PAIR], U32, name="slot_w", tag="words%d" % (g % 2), bufs=1, align_bytes=64)
             for s in range(PASSES):
                 nc.vector.tensor_copy(out=slot_w[g][:, s, :], in_=dy_w[:, s, :].bitcast(U32).indirect(entries(g)))
 
         def gather_scales(g):
-            slot_s[g] = slot_tile(g, 2, [P, PAIR], U8, "slot_s")
+            slot_s[g] = work.tile([P, PAIR], U8, name="slot_s", bufs=PAIRS, align_bytes=64)
             nc.vector.tensor_copy(out=slot_s[g][:], in_=dy_s[:].indirect(entries(g)))
 
         def first_product(e, s, acc, operand):
@@ -204,7 +203,10 @@ def tile_moe_adb_none_kernel(
                 gate_t = psum.tile([P, P], F32, name="gate_t", tag="turn")
                 nc.tensor.transpose(gate_t[:], gate_rows[:], ident[:])
             sums[e] = psum.tile([P, H], F32, name="acc", tag="acc", bufs=6)
-            grouped = rounded(raw[0], (LAST_WB_SCALAR_COLS if e == E - 1 else WB_SCALAR_COLS)[0], "wb_bf")
+            if e % 2 and 2 <= e // 2 + 1 < PAIRS:
+                grouped = rounded(raw[0], WB_SCALAR_COLS[0], "words%d" % ((e // 2 + 1) % 2), 1)
+            else:
+                grouped = rounded(raw[0], (LAST_WB_SCALAR_COLS if e == E - 1 else WB_SCALAR_COLS)[0], "wb_bf")
             if e > 1:
                 dh_bf = leave_turned(e - 2, turned)
             first_product(e, 0, sums[e], quantized(grouped, "wb"))
@@ -220,41 +222,57 @@ def tile_moe_adb_none_kernel(
                 turned = gate_and_turn(e - 1, sums[e - 1])
         quantize_dh(E - 2, leave_turned(E - 2, turned))
 
-        banks, dx, pair_sum = {}, {}, {}
+        banks, dx, pair_sum, picked = {}, {}, {}, {}
 
-        def second_product(c, g, grouped):
+        def dx_pass(target, codes, scales, i, e):
+            cols = slice(i * P, (i + 1) * P)
+            slots = slice(e * C, (e + 1) * C)
+            nc.tensor.matmul_mx(
+                out=target,
+                lhsT=codes[:, cols].bitcast(FP8X4),
+                lhsT_scale=scales[:, cols],
+                rhs=dh_codes[:, slots].bitcast(FP8X4),
+                rhs_scale=dh_scales[:, slots],
+                start=True,
+                stop=True,
+            )
+
+        dx_low = keep.tile([P, 2, SLOTS], F32, name="dx_low")
+        dx[0], dx[1] = dx_low[:, 0, :], dx_low[:, 1, :]
+        for e in range(E):
+            raw = staged([P, PACK, 2 * P], F32, "wa_raw")
+            nc.sync.dma_start(out=raw[:], in_=wat[e].rearrange("(p j) k -> p j k", j=PACK)[:, :, 0 : 2 * P])
+            grouped = rounded(raw[:], HALF_SHARE[e] * 64, "wa_bf")
+            if e == 0:
+                quantize_dh(E - 1, leave_turned(E - 1, gate_and_turn(E - 1, sums[E - 1])))
             codes, scales = quantized(grouped, "wa")
+            if e % 2 == 0:
+                bank = psum.tile([P, 2, 2, C], F32, name="dx_bank", tag="acc", bufs=6)
+            for i in range(2):
+                dx_pass(bank[:, i, e % 2, :], codes, scales, i, e)
+            if e % 2 == 1:
+                (nc.vector.tensor_copy if HALF_DX_ON_VECTOR[e // 2] else nc.scalar.copy)(
+                    out=dx_low[:, :, (e - 1) * C : (e + 1) * C], in_=bank[:].rearrange("p c e j -> p c (e j)")
+                )
+
+        def second_product(c, g, operand):
+            codes, scales = operand
             if g % 2 == 0:
                 banks[c, g // 2] = psum.tile([P, BANK], F32, name="dx_bank", tag="acc", bufs=6)
             for i in range(2):
-                cols = slice(i * P, (i + 1) * P)
-                slots = slice(g * PAIR + i * C, g * PAIR + (i + 1) * C)
                 place = (g % 2) * PAIR + i * C
-                nc.tensor.matmul_mx(
-                    out=banks[c, g // 2][:, place : place + C],
-                    lhsT=codes[:, cols].bitcast(FP8X4),
-                    lhsT_scale=scales[:, cols],
-                    rhs=dh_codes[:, slots].bitcast(FP8X4),
-                    rhs_scale=dh_scales[:, slots],
-                    start=True,
-                    stop=True,
-                )
+                dx_pass(banks[c, g // 2][:, place : place + C], codes, scales, i, 2 * g + i)
 
-        def leave_dx(c, b):
-            copy = nc.vector.tensor_copy if c == 0 and FIRST_DX_ON_VECTOR[b] else nc.scalar.copy
-            width = min(BANK, SLOTS - b * BANK)
-            if b == 0 and c == 0:
-                dx[c] = keep.tile([P, SLOTS], F32, name="dx")
-            elif b == 0:
-                dx[c] = after(DX_AFTER[c], [P, SLOTS], F32, "dx")
-            copy(out=dx[c][:, b * BANK : b * BANK + width], in_=banks[c, b][:, 0:width])
-
-        picked = {}
+        def leave_dx(c):
+            dx[c] = after(DX_AFTER[c - 2], [P, SLOTS], F32, "dx")[:]
+            for b in range(3):
+                width = min(BANK, SLOTS - b * BANK)
+                nc.scalar.copy(out=dx[c][:, b * BANK : b * BANK + width], in_=banks[c, b][:, 0:width])
 
         def pick(c, r):
             if r == 0:
                 picked[c] = work.tile([P, 2, T], F32, name="picked")
-            nc.vector.tensor_copy(out=picked[c][:, r, :], in_=dx[c][:].indirect(token_lists[r][:]))
+            nc.vector.tensor_copy(out=picked[c][:, r, :], in_=dx[c].indirect(token_lists[r][:]))
 
         def add_picked(c):
             pair_sum[c] = work.tile([P, T], F32, name="pair_sum", tag="late%d" % c, bufs=1, align_bytes=64)
@@ -262,46 +280,6 @@ def tile_moe_adb_none_kernel(
 
         def load_chunk(c):
             return [load_wa(c, 2 * g, 2 * g + 2)[0] for g in range(PAIRS)]
-
-        raw = load_chunk(0)
-        bf = [rounded(raw[0], FIRST_CHUNK_SCALAR_COLS[0], "wa_bf")]
-        turned = gate_and_turn(E - 1, sums[E - 1])
-        bf.append(rounded(raw[1], FIRST_CHUNK_SCALAR_COLS[1], "wa_bf"))
-        second_product(0, 0, bf[0])
-        dh_bf = leave_turned(E - 1, turned)
-        bf.append(rounded(raw[2], FIRST_CHUNK_SCALAR_COLS[2], "wa_bf"))
-        second_product(0, 1, bf[1])
-        quantize_dh(E - 1, dh_bf)
-        bf.append(rounded(raw[3], FIRST_CHUNK_SCALAR_COLS[3], "wa_bf"))
-        leave_dx(0, 0)
-        second_product(0, 2, bf[2])
-        bf.append(rounded(raw[4], FIRST_CHUNK_SCALAR_COLS[4], "wa_bf"))
-        second_product(0, 3, bf[3])
-        second_product(0, 4, bf[4])
-        leave_dx(0, 1)
-
-        leave_dx(0, 2)
-        raw = load_chunk(1)
-        ahead = rounded(raw[0], PAIR, "wa_bf")
-        for c in range(1, CHUNKS):
-            second_product(c, 0, ahead)
-            bf = [ahead] + [rounded(raw[g], PAIR, "wa_bf") for g in (1, 2, 3)]
-            pick(c - 1, 0)
-            second_product(c, 1, bf[1])
-            pick(c - 1, 1)
-            second_product(c, 2, bf[2])
-            bf.append(rounded(raw[4], 0, "late%d" % (c - 1), bufs=1))
-            second_product(c, 3, bf[3])
-            second_product(c, 4, bf[4])
-            if c + 1 < CHUNKS:
-                raw = load_chunk(c + 1)
-                ahead = rounded(raw[0], PAIR, "wa_bf")
-            else:
-                raw = load_wt(0) + load_wt(1)
-                wt_bf = [rounded(piece, 2 * P, "wa_bf") for piece in raw[0:1]]
-            for b in range(3):
-                leave_dx(c, b)
-            add_picked(c - 1)
 
         base = {}
 
@@ -329,24 +307,44 @@ def tile_moe_adb_none_kernel(
                     )
 
         def finish(c):
-            if c == 0:
-                result = after(DX_AFTER[last], [P, T], F32, "result")
-            elif c == 1:
+            if c == 0 and HOLD_RESULT[0]:
+                result = after(DX_AFTER[1], [P, T], F32, "result")
+            elif c == 1 and HOLD_RESULT[1]:
                 result = work.tile([P, T], F32, name="result", tag="last_bf", bufs=1, align_bytes=64)
             else:
-                result = work.tile([P, T], F32, name="result")
+                result = work.tile([P, T], F32, name="result", bufs=3)
             for part, tokens in zip(base[c], (slice(0, BANK), slice(BANK, T))):
                 nc.vector.tensor_tensor(out=result[:, tokens], in0=part, in1=pair_sum[c][:, tokens], op=ADD)
             nc.sync.dma_start(out=out[c * P : (c + 1) * P, :], in_=result[:])
 
         last = CHUNKS - 1
-        bf = wt_bf + [rounded(piece, 2 * P, "wa_bf") for piece in raw[1:3]] + [rounded(raw[3], 2 * P, "last_bf", bufs=1)]
-        frozen_pass(0, 0, quantized(bf[0], "wa"))
-        pick(last, 0)
-        frozen_pass(0, 1, quantized(bf[1], "wa"))
-        pick(last, 1)
-        frozen_pass(1, 0, quantized(bf[2], "wa"))
-        frozen_pass(1, 1, quantized(bf[3], "wa"))
-        add_picked(last)
+        raw = load_chunk(2) + load_chunk(3) + load_wt(0) + load_wt(1)
+        bf = {}
+
+        def round_unit(u):
+            if u in HOLD_SUM:
+                bf[u] = rounded(raw[u], UNIT_SHARE[u] * 64, "late%d" % HOLD_SUM.index(u), bufs=1)
+            elif u == len(raw) - 1:
+                bf[u] = rounded(raw[u], UNIT_SHARE[u] * 64, "last_bf", bufs=1)
+            else:
+                bf[u] = rounded(raw[u], UNIT_SHARE[u] * 64, "wa_bf")
+
+        round_unit(0)
+        for u in range(len(raw)):
+            if u + 1 < len(raw):
+                round_unit(u + 1)
+            operand = quantized(bf[u], "wa")
+            if u < 2 * PAIRS:
+                second_product(2 + u // PAIRS, u % PAIRS, operand)
+            else:
+                frozen_pass((u - 2 * PAIRS) // 2, u % 2, operand)
+            if u in (PAIRS - 1, 2 * PAIRS - 1):
+                leave_dx(2 + u // PAIRS)
+            for n, at in enumerate(PICK_AT):
+                if at == u:
+                    pick(n // 2, n % 2)
+            for c in range(CHUNKS):
+                if u == max(PICK_AT[2 * c + 1], HOLD_SUM[c] if c < last else 0):
+                    add_picked(c)
         for c in range(CHUNKS):
             finish(c)

from contextlib import ExitStack

import concourse.mybir as mybir
from concourse.masks import make_identity

K, T, E, C, H, N = 512, 640, 10, 128, 512, 1024
SLOTS = E * C
FLOPS = 2 * (N * K * T + N * H * SLOTS + H * K * SLOTS)

F32 = mybir.dt.float32
BF16 = mybir.dt.bfloat16
I32 = mybir.dt.int32
U32 = mybir.dt.uint32
U16 = mybir.dt.uint16
U8 = mybir.dt.uint8
FP8X4 = mybir.dt.float8_e4m3fn_x4
COPY = mybir.ActivationFunctionType.Copy
ADD = mybir.AluOpType.add

P = 128
PACK = 4
PASSES = N // (P * PACK)
CHUNKS = K // P
LIST_COL = 16
PAIR = 2 * C
PAIRS = E // 2
BANK = 512
TAIL = T - BANK
SCALE_ROWS = 4

STAGE_BUFS = 16
WB_SCALAR_COLS = (0, H)
LAST_WB_SCALAR_COLS = (0, 512)
LATE_TURN_ON_SCALAR = (1, 0)
HALF_SHARE = (2, 2, 0, 3, 0, 4, 1, 2, 4, 0)
HALF_DX_ON_VECTOR = (0, 1, 1, 0, 0)
UNIT_SHARE = (0, 3, 4, 4, 2, 4, 3, 3, 3, 4, 4, 2, 3, 4)
DX_AFTER = (35, 39)
HOLD_SUM = (3, 4, 9)
HOLD_RESULT = (1, 1)
PICK_AT = (0, 1, 2, 4, 5, 7, 9, 12)


def round_and_interleave(nc, grouped, raw, scalar_cols):
    width = raw.shape[2]
    shares = ((nc.scalar.copy, 0, scalar_cols), (nc.vector.tensor_copy, scalar_cols, width))
    for copy, first, last in shares:
        if first < last:
            copy(
                out=grouped[:, first:last, :].rearrange("p (c i) t -> p c t i", i=4),
                in_=raw[:, :, first:last].rearrange("p t (c i) -> p c t i", i=4),
            )


def quantize(nc, codes, scales, grouped):
    nc.vector.quantize_mx(out=codes.bitcast(FP8X4), scales=scales, in_=grouped.rearrange("p c t -> p (c t)"))


def tile_moe_adb_none_kernel(
    tc, dy_words, dy_scales, wt, wbt, wat, gate, offs, pos1, pos2, out
):
    nc = tc.nc
    with ExitStack() as ctx:
        keep = ctx.enter_context(tc.tile_pool(name="keep", bufs=1))
        stage = ctx.enter_context(tc.tile_pool(name="stage", bufs=1))
        work = ctx.enter_context(tc.tile_pool(name="work", bufs=2))
        psum = ctx.enter_context(tc.psum_pool(name="psum", bufs=2))

        slot_list = keep.tile([P, SLOTS // LIST_COL], U16, name="slot_list")
        token_lists = [keep.tile([P, T // LIST_COL], U16, name="token_list%d" % r) for r in range(2)]
        dy_w = keep.tile([P, PASSES, T], I32, name="dy_w", align_bytes=64)
        dy_s = keep.tile([P, T], U8, name="dy_s", align_bytes=64)
        dh_codes = keep.tile([P, SLOTS], U32, name="dh_codes", align_bytes=64)
        dh_scales = keep.tile([P, SLOTS], U8, name="dh_scales", align_bytes=64)
        ident = keep.tile([P, P], F32, name="ident")
        gate_rows = keep.tile([P, P], F32, name="gate_rows")
        gate_cols = keep.tile([P, E], F32, name="gate_cols")

        places = []

        def staged(shape, dtype, name):
            places.append("place%d" % (len(places) % STAGE_BUFS))
            return stage.tile(shape, dtype, name=name, tag=places[-1], align_bytes=64)

        def after(place, shape, dtype, name):
            return stage.tile(shape, dtype, name=name, tag=places[place], align_bytes=64)

        nc.vector.memset(dy_s[:].bitcast(I32), 0)
        make_identity(nc, ident[:])

        nc.sync.dma_start(out=slot_list[:], in_=offs)
        nc.sync.dma_start(out=dy_w[:], in_=dy_words.rearrange("s p t d -> p s (t d)").bitcast(I32))
        for q in range(4):
            nc.sync.dma_start(
                out=dy_s[32 * q : 32 * q + PASSES * SCALE_ROWS, :].bitcast(I32),
                in_=dy_scales[:, SCALE_ROWS * q : SCALE_ROWS * (q + 1), :].bitcast(I32),
            )
        small_loads = [
            (gate_rows[:], gate.rearrange("r (e u) -> (r e) u", u=C)[0:P, :]),
            (token_lists[0][:], pos1),
            (token_lists[1][:], pos2),
        ]

        def load_wb(e, s):
            raw = staged([P, PACK, H], F32, "wb_raw")
            nc.sync.dma_start(out=raw[:], in_=wbt[e].rearrange("(s p j) w -> s p j w", s=PASSES, j=PACK)[s])
            return raw[:]

        def load_wa(c, first, last):
            raw = staged([P, PACK, (last - first) * P], F32, "wa_raw")
            for e in range(first, last):
                nc.sync.dma_start(
                    out=raw[:, :, (e - first) * P : (e - first + 1) * P],
                    in_=wat[e].rearrange("(p j) k -> p j k", j=PACK)[:, :, c * P : (c + 1) * P],
                )
            return [raw[:, :, i * PAIR : (i + 1) * PAIR] for i in range((last - first) // 2)]

        def load_wt(h):
            raw = [staged([P, PACK, 2 * P], F32, "wt_raw") for s in range(PASSES)]
            for s in range(PASSES):
                nc.sync.dma_start(
                    out=raw[s][:],
                    in_=wt.rearrange("(s p j) k -> s p j k", s=PASSES, j=PACK)[s, :, :, h * 2 * P : (h + 1) * 2 * P],
                )
            return [piece[:] for piece in raw]

        def rounded(raw, scalar_cols, name, bufs=4):
            grouped = work.tile([P, raw.shape[2], PACK], BF16, name=name, bufs=bufs, align_bytes=64)
            round_and_interleave(nc, grouped[:], raw, scalar_cols)
            return grouped[:]

        def quantized(grouped, name):
            codes = work.tile([P, grouped.shape[1]], U32, name=name + "_codes", bufs=4, align_bytes=64)
            scales = work.tile([P, grouped.shape[1]], U8, name=name + "_scales", bufs=4, align_bytes=64)
            quantize(nc, codes[:], scales[:], grouped)
            return codes, scales

        slot_w, slot_s = {}, {}

        def entries(g):
            return slot_list[:, g * PAIR // LIST_COL : (g + 1) * PAIR // LIST_COL]

        def gather_words(g):
            slot_w[g] = work.tile([P, PASSES, PAIR], U32, name="slot_w", tag="words%d" % (g % 2), bufs=1, align_bytes=64)
            for s in range(PASSES):
                nc.vector.tensor_copy(out=slot_w[g][:, s, :], in_=dy_w[:, s, :].bitcast(U32).indirect(entries(g)))

        def gather_scales(g):
            slot_s[g] = work.tile([P, PAIR], U8, name="slot_s", bufs=PAIRS, align_bytes=64)
            nc.vector.tensor_copy(out=slot_s[g][:], in_=dy_s[:].indirect(entries(g)))

        def first_product(e, s, acc, operand):
            slots = slice(e % 2 * C, (e % 2 + 1) * C)
            codes, scales = operand
            nc.tensor.matmul_mx(
                out=acc[:],
                lhsT=slot_w[e // 2][:, s, slots].bitcast(FP8X4),
                lhsT_scale=slot_s[e // 2][SCALE_ROWS * s : P, slots],
                rhs=codes[:].bitcast(FP8X4),
                rhs_scale=scales[:],
                start=(s == 0),
                stop=(s == PASSES - 1),
            )

        def gate_and_turn(e, acc):
            if e + 1 < E:
                dh_rows = after(PASSES * (e + 1) + 1, [P, 2, P, 2], BF16, "dh_rows")
            else:
                dh_rows = work.tile([P, 2, P, 2], BF16, name="dh_rows", bufs=1, align_bytes=64)
            nc.scalar.activation(
                out=dh_rows[:],
                in_=acc[:].rearrange("j (p u v) -> j u p v", u=2, v=2),
                func=COPY,
                scale=gate_cols[:, e : e + 1],
            )
            pairs = dh_rows[:].rearrange("j u p v -> j (u p v)").bitcast(F32)
            turned = psum.tile([P, 2, C], F32, name="turned", tag="turn")
            for u in range(2):
                nc.tensor.transpose(turned[:, u, :], pairs[:, u * P : (u + 1) * P], ident[:])
            return turned

        def leave_turned(e, turned):
            dh_bf = work.tile([P, C, PACK], BF16, name="dh_bf", align_bytes=64)
            (nc.scalar.copy if e >= E - 2 and LATE_TURN_ON_SCALAR[e - E + 2] else nc.vector.tensor_copy)(
                out=dh_bf[:].rearrange("p j t -> p (j t)").bitcast(F32).rearrange("p (j u) -> p j u", u=2),
                in_=turned[:].rearrange("p u j -> p j u"),
            )
            return dh_bf

        def quantize_dh(e, dh_bf):
            slots = slice(e * C, (e + 1) * C)
            quantize(nc, dh_codes[:, slots], dh_scales[:, slots], dh_bf[:])

        for g in range(2):
            gather_words(g)
            gather_scales(g)
        sums = {}
        for e in range(E):
            raw = [load_wb(e, s) for s in range(PASSES)]
            if e < len(small_loads):
                nc.sync.dma_start(out=small_loads[e][0], in_=small_loads[e][1])
            if e == 0:
                gate_t = psum.tile([P, P], F32, name="gate_t", tag="turn")
                nc.tensor.transpose(gate_t[:], gate_rows[:], ident[:])
            sums[e] = psum.tile([P, H], F32, name="acc", tag="acc", bufs=6)
            if e % 2 and 2 <= e // 2 + 1 < PAIRS:
                grouped = rounded(raw[0], WB_SCALAR_COLS[0], "words%d" % ((e // 2 + 1) % 2), 1)
            else:
                grouped = rounded(raw[0], (LAST_WB_SCALAR_COLS if e == E - 1 else WB_SCALAR_COLS)[0], "wb_bf")
            if e > 1:
                dh_bf = leave_turned(e - 2, turned)
            first_product(e, 0, sums[e], quantized(grouped, "wb"))
            if e > 1:
                quantize_dh(e - 2, dh_bf)
            if 2 <= e // 2 + 1 < PAIRS:
                (gather_words if e % 2 else gather_scales)(e // 2 + 1)
            grouped = rounded(raw[1], (LAST_WB_SCALAR_COLS if e == E - 1 else WB_SCALAR_COLS)[1], "wb_bf")
            if e == 0:
                nc.scalar.activation(out=gate_cols[:], in_=gate_t[:, 0:E], func=COPY)
            first_product(e, 1, sums[e], quantized(grouped, "wb"))
            if e > 0:
                turned = gate_and_turn(e - 1, sums[e - 1])
        quantize_dh(E - 2, leave_turned(E - 2, turned))

        banks, dx, pair_sum, picked = {}, {}, {}, {}

        def dx_pass(target, codes, scales, i, e):
            cols = slice(i * P, (i + 1) * P)
            slots = slice(e * C, (e + 1) * C)
            nc.tensor.matmul_mx(
                out=target,
                lhsT=codes[:, cols].bitcast(FP8X4),
                lhsT_scale=scales[:, cols],
                rhs=dh_codes[:, slots].bitcast(FP8X4),
                rhs_scale=dh_scales[:, slots],
                start=True,
                stop=True,
            )

        dx_low = keep.tile([P, 2, SLOTS], F32, name="dx_low")
        dx[0], dx[1] = dx_low[:, 0, :], dx_low[:, 1, :]
        for e in range(E):
            raw = staged([P, PACK, 2 * P], F32, "wa_raw")
            nc.sync.dma_start(out=raw[:], in_=wat[e].rearrange("(p j) k -> p j k", j=PACK)[:, :, 0 : 2 * P])
            grouped = rounded(raw[:], HALF_SHARE[e] * 64, "wa_bf")
            if e == 0:
                quantize_dh(E - 1, leave_turned(E - 1, gate_and_turn(E - 1, sums[E - 1])))
            codes, scales = quantized(grouped, "wa")
            if e % 2 == 0:
                bank = psum.tile([P, 2, 2, C], F32, name="dx_bank", tag="acc", bufs=6)
            for i in range(2):
                dx_pass(bank[:, i, e % 2, :], codes, scales, i, e)
            if e % 2 == 1:
                (nc.vector.tensor_copy if HALF_DX_ON_VECTOR[e // 2] else nc.scalar.copy)(
                    out=dx_low[:, :, (e - 1) * C : (e + 1) * C], in_=bank[:].rearrange("p c e j -> p c (e j)")
                )

        def second_product(c, g, operand):
            codes, scales = operand
            if g % 2 == 0:
                banks[c, g // 2] = psum.tile([P, BANK], F32, name="dx_bank", tag="acc", bufs=6)
            for i in range(2):
                place = (g % 2) * PAIR + i * C
                dx_pass(banks[c, g // 2][:, place : place + C], codes, scales, i, 2 * g + i)

        def leave_dx(c):
            dx[c] = after(DX_AFTER[c - 2], [P, SLOTS], F32, "dx")[:]
            for b in range(3):
                width = min(BANK, SLOTS - b * BANK)
                nc.scalar.copy(out=dx[c][:, b * BANK : b * BANK + width], in_=banks[c, b][:, 0:width])

        def pick(c, r):
            if r == 0:
                picked[c] = work.tile([P, 2, T], F32, name="picked")
            nc.vector.tensor_copy(out=picked[c][:, r, :], in_=dx[c].indirect(token_lists[r][:]))

        def add_picked(c):
            pair_sum[c] = work.tile([P, T], F32, name="pair_sum", tag="late%d" % c, bufs=1, align_bytes=64)
            nc.vector.tensor_tensor(out=pair_sum[c][:], in0=picked[c][:, 0, :], in1=picked[c][:, 1, :], op=ADD)

        def load_chunk(c):
            return [load_wa(c, 2 * g, 2 * g + 2)[0] for g in range(PAIRS)]

        base = {}

        def frozen_pass(h, s, operand):
            codes, scales = operand
            for i in range(2):
                c = 2 * h + i
                cols = slice(i * P, (i + 1) * P)
                if s == 0:
                    wide = psum.tile([P, BANK], F32, name="acc", tag="acc", bufs=6)
                    if h == 0:
                        narrow = psum.tile([P, TAIL], F32, name="narrow", tag="turn")
                    else:
                        narrow = psum.tile([P, TAIL], F32, name="narrow", tag="acc", bufs=6)
                    base[c] = (wide[:], narrow[:])
                for target, tokens in zip(base[c], (slice(0, BANK), slice(BANK, T))):
                    nc.tensor.matmul_mx(
                        out=target,
                        lhsT=codes[:, cols].bitcast(FP8X4),
                        lhsT_scale=scales[:, cols],
                        rhs=dy_w[:, s, tokens].bitcast(FP8X4),
                        rhs_scale=dy_s[SCALE_ROWS * s : P, tokens],
                        start=(s == 0),
                        stop=(s == PASSES - 1),
                    )

        def finish(c):
            if c == 0 and HOLD_RESULT[0]:
                result = after(DX_AFTER[1], [P, T], F32, "result")
            elif c == 1 and HOLD_RESULT[1]:
                result = work.tile([P, T], F32, name="result", tag="last_bf", bufs=1, align_bytes=64)
            else:
                result = work.tile([P, T], F32, name="result", bufs=3)
            for part, tokens in zip(base[c], (slice(0, BANK), slice(BANK, T))):
                nc.vector.tensor_tensor(out=result[:, tokens], in0=part, in1=pair_sum[c][:, tokens], op=ADD)
            nc.sync.dma_start(out=out[c * P : (c + 1) * P, :], in_=result[:])

        last = CHUNKS - 1
        raw = load_chunk(2) + load_chunk(3) + load_wt(0) + load_wt(1)
        bf = {}

        def round_unit(u):
            if u in HOLD_SUM:
                bf[u] = rounded(raw[u], UNIT_SHARE[u] * 64, "late%d" % HOLD_SUM.index(u), bufs=1)
            elif u == len(raw) - 1:
                bf[u] = rounded(raw[u], UNIT_SHARE[u] * 64, "last_bf", bufs=1)
            else:
                bf[u] = rounded(raw[u], UNIT_SHARE[u] * 64, "wa_bf")

        round_unit(0)
        for u in range(len(raw)):
            if u + 1 < len(raw):
                round_unit(u + 1)
            operand = quantized(bf[u], "wa")
            if u < 2 * PAIRS:
                second_product(2 + u // PAIRS, u % PAIRS, operand)
            else:
                frozen_pass((u - 2 * PAIRS) // 2, u % 2, operand)
            if u in (PAIRS - 1, 2 * PAIRS - 1):
                leave_dx(2 + u // PAIRS)
            for n, at in enumerate(PICK_AT):
                if at == u:
                    pick(n // 2, n % 2)
            for c in range(CHUNKS):
                if u == max(PICK_AT[2 * c + 1], HOLD_SUM[c] if c < last else 0):
                    add_picked(c)
        for c in range(CHUNKS):
            finish(c)
